import numpy as np
import ml_dtypes


def mxq(x, axis, fmt="e4m3"):
    dtype, down = {"e4m3": (ml_dtypes.float8_e4m3fn, 7), "e5m2": (ml_dtypes.float8_e5m2, 14)}[fmt]
    v = np.moveaxis(np.asarray(x, np.float32).astype(ml_dtypes.bfloat16).astype(np.float64), axis, -1)
    blocks = v.reshape(v.shape[:-1] + (-1, 32))
    amax = np.abs(blocks).max(-1, keepdims=True)
    byte = np.maximum(np.where(amax > 0, np.frexp(amax)[1] - 1 + 127, 0) - down, 1)
    scale = np.exp2(byte - 127.0)
    codes = (blocks / scale).astype(np.float32).astype(dtype).astype(np.float64)
    return np.moveaxis((codes * scale).reshape(v.shape), -1, axis)


WIDE = False


def mx_kscale(k):
    if not WIDE:
        return np.ones(k)
    levels = np.array([10, -10, 5, -5, 0])
    if k % 512:
        return np.exp2(np.random.permutation(np.resize(levels, k // 32))).repeat(32)
    a = np.empty((k // 512, 16))
    for p in range(k // 512):
        a[p, :8] = np.random.permutation(np.resize(levels, 8))
        for g in range(8):
            far = levels[np.abs(levels - a[p, g]) >= 10]
            a[p, g + 8] = far[np.random.randint(len(far))]
    return np.exp2(a.ravel()).repeat(32)


def f64(x):
    return np.asarray(x).astype(np.float64)


def striped(idx):
    return np.tile(np.asarray(idx).reshape(-1, 16).T, (8, 1)).astype(np.uint16)


def unstriped(offs):
    return offs[:16].T.reshape(-1).astype(np.int64)


E2M1 = np.array([0.0, 0.5, 1.0, 1.5, 2.0, 3.0, 4.0, 6.0, -0.0, -0.5, -1.0, -1.5, -2.0, -3.0, -4.0, -6.0])


def pack_weight(w, fmt):
    k, n = w.shape
    w = f64(np.asarray(w, np.float32).astype(ml_dtypes.bfloat16)).reshape(k // 32, 32, n)
    amax = np.abs(w).max(1)
    if fmt == "e4m3":
        byte = np.frexp(amax)[1] - 1 + 127 - 7
    else:
        mant, ex = np.frexp(amax / 6.0)
        byte = np.where(mant > 0.5, ex, ex - 1) + 127
    byte = np.clip(np.where(amax > 0, byte, 1), 1, 254)
    scaled = (w * np.exp2(127.0 - byte)[:, None, :]).reshape(k, n).astype(np.float32)
    by_word = np.ascontiguousarray(scaled.reshape(k // 512, 128, 4, n).transpose(0, 1, 3, 2))
    if fmt == "e4m3":
        words = by_word.astype(ml_dtypes.float8_e4m3fn).view(np.uint8)
    else:
        c = by_word.astype(ml_dtypes.float4_e2m1fn).view(np.uint8) & 0xF
        words = (c[..., 0::2] | (c[..., 1::2] << 4)).reshape(k // 512, 128, 2 * n)
    return np.ascontiguousarray(words), np.ascontiguousarray(byte.astype(np.uint8).reshape(k // 512, 16, n))


def unpack_weight(words, scales, fmt):
    g, _, n = scales.shape
    words = np.ascontiguousarray(words).reshape(g, 128, n, -1)
    if fmt == "e4m3":
        vals = words.view(ml_dtypes.float8_e4m3fn).astype(np.float64)
    else:
        nib = np.empty((g, 128, n, 4), np.uint8)
        nib[..., 0::2] = words & 0xF
        nib[..., 1::2] = words >> 4
        vals = E2M1[nib]
    vals = vals * np.repeat(np.exp2(scales.astype(np.float64) - 127.0), 8, axis=1)[..., None]
    return vals.transpose(0, 1, 3, 2).reshape(g * 512, n)


def bf(x):
    return np.asarray(x, np.float32).astype(ml_dtypes.bfloat16)


def planes(Y):
    r, m = Y.shape
    b = f64(bf(Y)).reshape(r // 32, 32, m)
    amax = np.abs(b).max(1)
    byte = np.clip(np.where(amax > 0, np.frexp(amax)[1] - 1 + 127 - 7, 1), 1, 254)
    codes = (b * np.exp2(127.0 - byte)[:, None, :]).reshape(r, m).astype(np.float32).astype(ml_dtypes.float8_e4m3fn).view(np.uint8)
    words = codes.reshape(r // 512, 128, 4, m).transpose(0, 1, 3, 2)
    return np.ascontiguousarray(words), np.ascontiguousarray(byte.astype(np.uint8).reshape(r // 512, 16, m))


D, E, T, I, Q = 512, 512, 2048, 512, 256


def setup_inputs():
    n = np.random.standard_normal
    idx = np.random.permutation(T)[:I]
    fd = mx_kscale(D)
    fi = mx_kscale(I)
    ti = np.ones(T)
    ti[idx] = fi
    keysp = pack_weight(n((D, T)) / fd[:, None], "e4m3")
    return {
        "query": (n((D, Q)) * 0.7 / np.sqrt(D) * fd[:, None]).astype(np.float32),
        "query2": (n((D, Q)) * 0.7 / np.sqrt(D) * fd[:, None]).astype(np.float32),
        "keys_words": keysp[0],
        "keys_scales": keysp[1],
        "sharp": (np.random.uniform(0.3, 1.2, (Q, 1))).astype(np.float32),
        "os": (np.random.uniform(4.0, 16.0, (1, I)) * fi).astype(np.float32),
        "vals": (n((E, T)) / ti).astype(np.float32),
        "offs": striped(idx),
    }


def reference(query, query2, keys_words, keys_scales, sharp, os, vals, offs):
    idx = unstriped(offs)
    keysu = unpack_weight(keys_words, keys_scales, "e4m3")
    queryq = mxq(f64(query), 0, "e4m3")
    keysidxg = keysu[:, idx]
    a = queryq.T @ keysidxg
    query2q = mxq(f64(query2), 0, "e4m3")
    b = query2q.T @ keysidxg
    dl = a - b
    p = np.exp(a * 0.5) / (np.square(dl) * f64(sharp) + 1.0)
    z = np.sum(p, axis=1, keepdims=True)
    w = p / z
    wo1 = w * f64(os)
    wt1 = wo1.T
    vt1 = f64(vals)[:, idx].T
    vt1q = mxq(vt1, 0, "e4m3")
    wt1q = mxq(wt1, 0, "e4m3")
    o = vt1q.T @ wt1q
    words, scales = planes(o)
    return o, words, scales

@@ -1,0 +1,193 @@
+from contextlib import ExitStack
+
+import concourse.mybir as mybir
+from concourse.masks import make_identity
+
+D, E, T, I, Q = 512, 512, 2048, 512, 256
+FLOPS = 2 * (2 * D * Q * I + I * E * Q)
+
+F32 = mybir.dt.float32
+BF16 = mybir.dt.bfloat16
+I32 = mybir.dt.int32
+U32 = mybir.dt.uint32
+U16 = mybir.dt.uint16
+U8 = mybir.dt.uint8
+FP8X4 = mybir.dt.float8_e4m3fn_x4
+ALU = mybir.AluOpType
+ACT = mybir.ActivationFunctionType
+
+P = 128
+PACK = 4
+HALVES = Q // P
+
+
+def tile_attend_alikescores_pl_kernel(tc, query, query2, keys_words, keys_scales, sharp, slot_factor, vals, offs, out_0, out_1, out_2):
+    nc = tc.nc
+    with ExitStack() as ctx:
+        sb = ctx.enter_context(tc.tile_pool(name="sb", bufs=1))
+        ps = ctx.enter_context(tc.psum_pool(name="ps", bufs=1))
+
+        def sbuf(name, shape, dtype, tag=None):
+            return sb.tile(shape, dtype, name=name, tag=tag or name, align_bytes=64)
+
+        offsets = sb.tile([P, I // 16], U16, name="offsets")
+        nc.sync.dma_start(offsets[:], offs)
+
+        key_scale_pool = sbuf("key_scale_pool", [P, T], U8)
+        nc.gpsimd.memset(key_scale_pool[:].bitcast(I32), 0)
+        for quad in range(4):
+            nc.scalar.dma_start(
+                key_scale_pool[32 * quad : 32 * quad + 4, :].bitcast(I32),
+                keys_scales[0][4 * quad : 4 * quad + 4, :].bitcast(I32),
+            )
+        q_raw = sbuf("q_raw", [P, PACK, Q], F32)
+        nc.sync.dma_start(q_raw[:], query.rearrange("(p t) q -> p t q", t=PACK))
+        key_word_pool = sbuf("key_word_pool", [P, T], U32)
+        nc.sync.dma_start(key_word_pool[:].bitcast(I32), keys_words[0].rearrange("p n t -> p (n t)").bitcast(I32))
+        q2_raw = sbuf("q2_raw", [P, PACK, Q], F32)
+        nc.sync.dma_start(q2_raw[:], query2.rearrange("(p t) q -> p t q", t=PACK))
+
+        ident = sbuf("ident", [P, P], F32)
+        make_identity(nc, ident[:])
+
+        sharp_col = sbuf("sharp_col", [P, HALVES], F32)
+        with nc.allow_non_contiguous_dma(reason="one value a partition"):
+            nc.gpsimd.dma_start(sharp_col[:], sharp.rearrange("(h p) o -> p (h o)", p=P))
+        os_col = sbuf("os_col", [P, PACK], F32)
+        nc.gpsimd.dma_start(os_col[:], slot_factor.rearrange("o (s t) -> s (o t)", t=PACK))
+
+        warm_in = sbuf("warm_in", [P, 1], F32)
+        warm_out = sbuf("warm_out", [P, 1], F32)
+        nc.vector.memset(warm_in[:], 1.0)
+        nc.scalar.activation(warm_out[:], warm_in[:], ACT.Ln)
+
+        key_scales = sbuf("key_scales", [P, I], U8)
+        nc.vector.tensor_copy(key_scales[:], key_scale_pool[:].indirect(offsets[:]))
+        key_words = sbuf("key_words", [P, I], U32, tag="key_scale_pool")
+        nc.vector.tensor_copy(key_words[:], key_word_pool[:].indirect(offsets[:]))
+
+        def quantise_queries(name, raw, sign, first_tag=None):
+            view = raw[:].rearrange("p t q -> p q t")
+            rounded = [sbuf(f"{name}_bf0", [P, P, PACK], BF16, tag=first_tag), sbuf(f"{name}_bf1", [P, P, PACK], BF16)]
+            nc.vector.tensor_scalar(rounded[0][:], view[:, 0:P, :], sign, None, ALU.mult)
+            nc.scalar.activation(rounded[1][:], view[:, P:Q, :], ACT.Copy, scale=sign)
+            operands = []
+            for h in range(HALVES):
+                codes = sbuf(f"{name}_codes{h}", [P, P], U32)
+                scales = sbuf(f"{name}_scales{h}", [P, P], U8)
+                nc.vector.quantize_mx(codes[:].bitcast(FP8X4), scales[:], rounded[h][:].rearrange("p q t -> p (q t)"))
+                operands.append((codes, scales))
+            return operands
+
+        def score_pass(bank, operand, start, stop):
+            codes, scales = operand
+            nc.tensor.matmul_mx(
+                bank[:], lhsT=codes[:].bitcast(FP8X4), lhsT_scale=scales[:],
+                rhs=key_words[:].bitcast(FP8X4), rhs_scale=key_scales[:], start=start, stop=stop,
+            )
+
+        q_mx = quantise_queries("q", q_raw, 1.0)
+        neg_q2_mx = quantise_queries("neg_q2", q2_raw, -1.0, "key_word_pool")
+
+        val_pool = []
+        for r, tag in enumerate(["q_raw", "q_bf0", "q_bf1", "q2_raw"]):
+            pool_r = sbuf(f"val_pool{r}", [P, T], F32, tag=tag)
+            nc.sync.dma_start(pool_r[:], vals.rearrange("(p r) t -> p r t", r=PACK)[:, r, :])
+            val_pool.append(pool_r)
+
+        a = [ps.tile([P, I], F32, name=f"bank_a{h}") for h in range(HALVES)]
+        neg_b0 = ps.tile([P, I], F32, name="bank_neg_b0")
+        dl1 = ps.tile([P, I], F32, name="bank_dl1")
+        score_pass(a[0], q_mx[0], True, True)
+        score_pass(dl1, q_mx[1], True, False)
+        score_pass(neg_b0, neg_q2_mx[0], True, True)
+        score_pass(dl1, neg_q2_mx[1], False, True)
+        score_pass(a[1], q_mx[1], True, True)
+
+        os_rows = ps.tile([P, PACK, P], F32, name="os_rows")
+        for t in range(PACK):
+            nc.tensor.transpose(os_rows[:, t, :], os_col[:, t : t + 1].to_broadcast([P, P]), ident[:])
+
+        neg_half_a = [sbuf(f"neg_half_a{h}", [P, I], F32) for h in range(HALVES)]
+        shift = [sbuf(f"shift{h}", [P, 1], F32) for h in range(HALVES)]
+        half_dl0 = sbuf("half_dl0", [P, I], F32)
+        dl_sq = [sbuf(f"dl_sq{h}", [P, I], F32) for h in range(HALVES)]
+        log_den = [sbuf(f"log_den{h}", [P, I], F32) for h in range(HALVES)]
+        neg_logit = [sbuf(f"neg_logit{h}", [P, I], F32) for h in range(HALVES)]
+        part = [sbuf(f"part{h}", [P, I], F32) for h in range(HALVES)]
+        z = [sbuf(f"z{h}", [P, 1], F32) for h in range(HALVES)]
+        inv_z = [sbuf(f"inv_z{h}", [P, 1], F32) for h in range(HALVES)]
+        w_bf = [sbuf(f"w_bf{h}", [P, I], BF16) for h in range(HALVES)]
+
+        nc.vector.tensor_scalar(neg_half_a[0][:], a[0][:], -0.5, None, ALU.mult, ALU.min, accum_out=shift[0][:])
+        nc.vector.scalar_tensor_tensor(half_dl0[:], neg_b0[:], -0.5, neg_half_a[0][:], ALU.mult, ALU.add)
+        nc.vector.tensor_scalar(neg_half_a[1][:], a[1][:], -0.5, None, ALU.mult, ALU.min, accum_out=shift[1][:])
+        nc.scalar.activation(dl_sq[0][:], half_dl0[:], ACT.Square, scale=2.0)
+        nc.scalar.activation(dl_sq[1][:], dl1[:], ACT.Square)
+        for h in range(HALVES):
+            nc.scalar.activation(log_den[h][:], dl_sq[h][:], ACT.Ln, bias=1.0, scale=sharp_col[:, h : h + 1])
+        for h in range(HALVES):
+            nc.vector.tensor_tensor(neg_logit[h][:], neg_half_a[h][:], log_den[h][:], ALU.add)
+        for h in range(HALVES):
+            nc.scalar.activation(part[h][:], neg_logit[h][:], ACT.Exp, bias=shift[h][:], scale=-1.0, accum_out=z[h][:])
+        for h in range(HALVES):
+            nc.vector.reciprocal(inv_z[h][:], z[h][:])
+            nc.vector.scalar_tensor_tensor(
+                w_bf[h][:].rearrange("q (s t) -> q s t", t=PACK), part[h][:].rearrange("q (s t) -> q s t", t=PACK),
+                inv_z[h][:], os_rows[:].rearrange("q t s -> q s t"), ALU.mult, ALU.mult,
+            )
+
+        def turn(name, rows_bf, bank_tag, sbuf_tag=None):
+            words = rows_bf[:].bitcast(F32)
+            turned = ps.tile([P, 2, P], F32, name=f"{name}_turned", tag=bank_tag)
+            for u in range(2):
+                nc.tensor.transpose(turned[:, u, :], words[:, u : 2 * P : 2], ident[:])
+            packed = sbuf(f"{name}_packed", [P, P * PACK], BF16, tag=sbuf_tag)
+            nc.scalar.copy(packed[:].bitcast(F32).rearrange("s (c u) -> s c u", u=2), turned[:].rearrange("s u c -> s c u"))
+            return packed
+
+        w_codes = sbuf("w_codes", [P, Q], U32)
+        w_scales = sbuf("w_scales", [P, Q], U8)
+        for h, bank_tag in enumerate(["bank_neg_b0", "bank_dl1"]):
+            packed = turn(f"w{h}", w_bf[h], bank_tag)
+            cols = slice(h * P, (h + 1) * P)
+            nc.vector.quantize_mx(w_codes[:, cols].bitcast(FP8X4), w_scales[:, cols], packed[:])
+
+        picked_tag = ["neg_q2_codes0", "log_den1", "q_bf0", "part1"]
+        packed_tag = ["neg_logit0", "neg_logit1", None, None]
+        turn_bank = ["bank_x0", "bank_x1", "bank_x2", "bank_a0"]
+        acc_bank = ["bank_a1", "bank_x0", "bank_x1", "bank_x2"]
+        v_mx = []
+        for r in range(PACK):
+            picked = sbuf(f"picked{r}", [P, I], BF16, tag=picked_tag[r])
+            nc.vector.tensor_copy(picked[:], val_pool[r][:].indirect(offsets[:]))
+            packed = turn(f"v{r}", picked, turn_bank[r], packed_tag[r])
+            codes = sbuf(f"v_codes{r}", [P, P], U32)
+            scales = sbuf(f"v_scales{r}", [P, P], U8)
+            nc.vector.quantize_mx(codes[:].bitcast(FP8X4), scales[:], packed[:])
+            v_mx.append((codes, scales))
+
+        result = sbuf("result", [P, PACK, Q], F32)
+        out_rows = out_0.rearrange("(p r) q -> p r q", r=PACK)
+        for r in range(PACK):
+            acc = ps.tile([P, Q], F32, name=f"acc{r}", tag=acc_bank[r])
+            codes, scales = v_mx[r]
+            nc.tensor.matmul_mx(
+                acc[:], lhsT=codes[:].bitcast(FP8X4), lhsT_scale=scales[:],
+                rhs=w_codes[:].bitcast(FP8X4), rhs_scale=w_scales[:], start=True, stop=True,
+            )
+            nc.scalar.copy(result[:, r, :], acc[:])
+            nc.sync.dma_start(out_rows[:, r, :], result[:, r, :])
+
+        result_bf = sbuf("result_bf", [P, Q, PACK], BF16)
+        nc.vector.tensor_copy(result_bf[:], result[:].rearrange("p r q -> p q r"))
+        out_codes = sbuf("out_codes", [P, Q], U32)
+        out_scales = sbuf("out_scales", [P, Q], U8)
+        nc.vector.quantize_mx(out_codes[:].bitcast(FP8X4), out_scales[:], result_bf[:].rearrange("p q r -> p (q r)"))
+        nc.sync.dma_start(out_1[0].rearrange("p c t -> p (c t)").bitcast(I32), out_codes[:].bitcast(I32))
+        for quad in range(4):
+            queue = nc.scalar if quad % 2 else nc.sync
+            queue.dma_start(
+                out_2[0][4 * quad : 4 * quad + 4, :].bitcast(I32),
+                out_scales[32 * quad : 32 * quad + 4, :].bitcast(I32),
+            )

@@ -33,28 +33,33 @@ def tile_attend_alikescores_pl_kernel(tc, query, query2, keys_words, keys_scales
         offsets = sb.tile([P, I // 16], U16, name="offsets")
         nc.sync.dma_start(offsets[:], offs)
 
+        q_raw = sbuf("q_raw", [P, PACK, Q], F32)
+        nc.sync.dma_start(q_raw[:], query.rearrange("(p t) q -> p t q", t=PACK))
         key_scale_pool = sbuf("key_scale_pool", [P, T], U8)
         nc.gpsimd.memset(key_scale_pool[:].bitcast(I32), 0)
         for quad in range(4):
-            nc.scalar.dma_start(
+            nc.sync.dma_start(
                 key_scale_pool[32 * quad : 32 * quad + 4, :].bitcast(I32),
                 keys_scales[0][4 * quad : 4 * quad + 4, :].bitcast(I32),
             )
-        q_raw = sbuf("q_raw", [P, PACK, Q], F32)
-        nc.sync.dma_start(q_raw[:], query.rearrange("(p t) q -> p t q", t=PACK))
         key_word_pool = sbuf("key_word_pool", [P, T], U32)
         nc.sync.dma_start(key_word_pool[:].bitcast(I32), keys_words[0].rearrange("p n t -> p (n t)").bitcast(I32))
         q2_raw = sbuf("q2_raw", [P, PACK, Q], F32)
         nc.sync.dma_start(q2_raw[:], query2.rearrange("(p t) q -> p t q", t=PACK))
+        sharp_col = sbuf("sharp_col", [P, HALVES], F32)
+        with nc.allow_non_contiguous_dma(reason="one value a partition"):
+            nc.sync.dma_start(sharp_col[:], sharp.rearrange("(h p) o -> p (h o)", p=P))
+
+        val_pool = [sbuf(f"val_pool{r}", [P, T], F32) for r in range(PACK)]
+        val_rows = vals.rearrange("(p r) t -> p r t", r=PACK)
+        nc.sync.dma_start(val_pool[0][:], val_rows[:, 0, :])
+        os_col = sbuf("os_col", [P, PACK], F32)
+        nc.sync.dma_start(os_col[:], slot_factor.rearrange("o (s t) -> s (o t)", t=PACK))
+        for r in range(1, PACK):
+            nc.sync.dma_start(val_pool[r][:], val_rows[:, r, :])
 
         ident = sbuf("ident", [P, P], F32)
         make_identity(nc, ident[:])
-
-        sharp_col = sbuf("sharp_col", [P, HALVES], F32)
-        with nc.allow_non_contiguous_dma(reason="one value a partition"):
-            nc.gpsimd.dma_start(sharp_col[:], sharp.rearrange("(h p) o -> p (h o)", p=P))
-        os_col = sbuf("os_col", [P, PACK], F32)
-        nc.gpsimd.dma_start(os_col[:], slot_factor.rearrange("o (s t) -> s (o t)", t=PACK))
 
         warm_in = sbuf("warm_in", [P, 1], F32)
         warm_out = sbuf("warm_out", [P, 1], F32)
@@ -63,12 +68,12 @@ def tile_attend_alikescores_pl_kernel(tc, query, query2, keys_words, keys_scales
 
         key_scales = sbuf("key_scales", [P, I], U8)
         nc.vector.tensor_copy(key_scales[:], key_scale_pool[:].indirect(offsets[:]))
-        key_words = sbuf("key_words", [P, I], U32, tag="key_scale_pool")
+        key_words = sbuf("key_words", [P, I], U32)
         nc.vector.tensor_copy(key_words[:], key_word_pool[:].indirect(offsets[:]))
 
-        def quantise_queries(name, raw, sign, first_tag=None):
+        def quantise_queries(name, raw, sign):
             view = raw[:].rearrange("p t q -> p q t")
-            rounded = [sbuf(f"{name}_bf0", [P, P, PACK], BF16, tag=first_tag), sbuf(f"{name}_bf1", [P, P, PACK], BF16)]
+            rounded = [sbuf(f"{name}_bf{h}", [P, P, PACK], BF16) for h in range(HALVES)]
             nc.vector.tensor_scalar(rounded[0][:], view[:, 0:P, :], sign, None, ALU.mult)
             nc.scalar.activation(rounded[1][:], view[:, P:Q, :], ACT.Copy, scale=sign)
             operands = []
@@ -87,107 +92,106 @@ def tile_attend_alikescores_pl_kernel(tc, query, query2, keys_words, keys_scales
             )
 
         q_mx = quantise_queries("q", q_raw, 1.0)
-        neg_q2_mx = quantise_queries("neg_q2", q2_raw, -1.0, "key_word_pool")
+        neg_q2_mx = quantise_queries("neg_q2", q2_raw, -1.0)
 
-        val_pool = []
-        for r, tag in enumerate(["q_raw", "q_bf0", "q_bf1", "q2_raw"]):
-            pool_r = sbuf(f"val_pool{r}", [P, T], F32, tag=tag)
-            nc.sync.dma_start(pool_r[:], vals.rearrange("(p r) t -> p r t", r=PACK)[:, r, :])
-            val_pool.append(pool_r)
-
-        a = [ps.tile([P, I], F32, name=f"bank_a{h}") for h in range(HALVES)]
+        a0 = ps.tile([P, I], F32, name="bank_a0")
         neg_b0 = ps.tile([P, I], F32, name="bank_neg_b0")
         dl1 = ps.tile([P, I], F32, name="bank_dl1")
-        score_pass(a[0], q_mx[0], True, True)
-        score_pass(dl1, q_mx[1], True, False)
+        score_pass(a0, q_mx[0], True, True)
         score_pass(neg_b0, neg_q2_mx[0], True, True)
-        score_pass(dl1, neg_q2_mx[1], False, True)
-        score_pass(a[1], q_mx[1], True, True)
+        score_pass(dl1, neg_q2_mx[1], True, False)
+        score_pass(dl1, q_mx[1], False, True)
 
         os_rows = ps.tile([P, PACK, P], F32, name="os_rows")
         for t in range(PACK):
             nc.tensor.transpose(os_rows[:, t, :], os_col[:, t : t + 1].to_broadcast([P, P]), ident[:])
 
-        neg_half_a = [sbuf(f"neg_half_a{h}", [P, I], F32) for h in range(HALVES)]
+        neg_half_a = [sbuf(f"neg_half_a{h}", [P, I], F32, tag=["neg_q2_bf1", "val_pool0"][h]) for h in range(HALVES)]
         shift = [sbuf(f"shift{h}", [P, 1], F32) for h in range(HALVES)]
         half_dl0 = sbuf("half_dl0", [P, I], F32)
         dl_sq = [sbuf(f"dl_sq{h}", [P, I], F32) for h in range(HALVES)]
         log_den = [sbuf(f"log_den{h}", [P, I], F32) for h in range(HALVES)]
-        neg_logit = [sbuf(f"neg_logit{h}", [P, I], F32) for h in range(HALVES)]
         part = [sbuf(f"part{h}", [P, I], F32) for h in range(HALVES)]
-        z = [sbuf(f"z{h}", [P, 1], F32) for h in range(HALVES)]
-        inv_z = [sbuf(f"inv_z{h}", [P, 1], F32) for h in range(HALVES)]
+        z = sbuf("z", [P, HALVES], F32)
         w_bf = [sbuf(f"w_bf{h}", [P, I], BF16) for h in range(HALVES)]
 
-        nc.vector.tensor_scalar(neg_half_a[0][:], a[0][:], -0.5, None, ALU.mult, ALU.min, accum_out=shift[0][:])
+        nc.vector.tensor_scalar(neg_half_a[0][:], a0[:], -0.5, None, ALU.mult, ALU.min, accum_out=shift[0][:])
         nc.vector.scalar_tensor_tensor(half_dl0[:], neg_b0[:], -0.5, neg_half_a[0][:], ALU.mult, ALU.add)
-        nc.vector.tensor_scalar(neg_half_a[1][:], a[1][:], -0.5, None, ALU.mult, ALU.min, accum_out=shift[1][:])
+        a1 = ps.tile([P, I], F32, name="a1", tag="bank_neg_b0")
+        score_pass(a1, q_mx[1], True, True)
+        nc.vector.tensor_scalar(neg_half_a[1][:], a1[:], -0.5, None, ALU.mult, ALU.min, accum_out=shift[1][:])
         nc.scalar.activation(dl_sq[0][:], half_dl0[:], ACT.Square, scale=2.0)
         nc.scalar.activation(dl_sq[1][:], dl1[:], ACT.Square)
         for h in range(HALVES):
             nc.scalar.activation(log_den[h][:], dl_sq[h][:], ACT.Ln, bias=1.0, scale=sharp_col[:, h : h + 1])
+        picked = [sbuf(f"picked{r}", [P, I], BF16) for r in range(PACK)]
+        for r in range(PACK):
+            nc.vector.tensor_copy(picked[r][:], val_pool[r][:].indirect(offsets[:]))
+        neg_logit = sbuf("neg_logit", [P, HALVES * I], F32, tag="val_pool1")
+        inv_z = sbuf("inv_z", [P, HALVES], F32, tag="val_pool2")
         for h in range(HALVES):
-            nc.vector.tensor_tensor(neg_logit[h][:], neg_half_a[h][:], log_den[h][:], ALU.add)
+            nc.vector.tensor_tensor(neg_logit[:, h * I : (h + 1) * I], neg_half_a[h][:], log_den[h][:], ALU.add)
         for h in range(HALVES):
-            nc.scalar.activation(part[h][:], neg_logit[h][:], ACT.Exp, bias=shift[h][:], scale=-1.0, accum_out=z[h][:])
+            nc.scalar.activation(part[h][:], neg_logit[:, h * I : (h + 1) * I], ACT.Exp, bias=shift[h][:], scale=-1.0, accum_out=z[:, h : h + 1])
+        nc.vector.reciprocal(inv_z[:], z[:])
         for h in range(HALVES):
-            nc.vector.reciprocal(inv_z[h][:], z[h][:])
             nc.vector.scalar_tensor_tensor(
                 w_bf[h][:].rearrange("q (s t) -> q s t", t=PACK), part[h][:].rearrange("q (s t) -> q s t", t=PACK),
-                inv_z[h][:], os_rows[:].rearrange("q t s -> q s t"), ALU.mult, ALU.mult,
+                inv_z[:, h : h + 1], os_rows[:].rearrange("q t s -> q s t"), ALU.mult, ALU.mult,
             )
 
-        def turn(name, rows_bf, bank_tag, sbuf_tag=None):
+        def turn(name, rows_bf, bank_tag, packed):
             words = rows_bf[:].bitcast(F32)
             turned = ps.tile([P, 2, P], F32, name=f"{name}_turned", tag=bank_tag)
             for u in range(2):
                 nc.tensor.transpose(turned[:, u, :], words[:, u : 2 * P : 2], ident[:])
-            packed = sbuf(f"{name}_packed", [P, P * PACK], BF16, tag=sbuf_tag)
-            nc.scalar.copy(packed[:].bitcast(F32).rearrange("s (c u) -> s c u", u=2), turned[:].rearrange("s u c -> s c u"))
-            return packed
+            nc.scalar.copy(packed.bitcast(F32).rearrange("s (c u) -> s c u", u=2), turned[:].rearrange("s u c -> s c u"))
 
-        w_codes = sbuf("w_codes", [P, Q], U32)
+        slot_codes = sbuf("slot_codes", [P, Q + E], U32, tag="val_pool3")
         w_scales = sbuf("w_scales", [P, Q], U8)
         for h, bank_tag in enumerate(["bank_neg_b0", "bank_dl1"]):
-            packed = turn(f"w{h}", w_bf[h], bank_tag)
+            packed = sbuf(f"w_packed{h}", [P, I], BF16)
+            turn(f"w{h}", w_bf[h], bank_tag, packed[:])
             cols = slice(h * P, (h + 1) * P)
-            nc.vector.quantize_mx(w_codes[:, cols].bitcast(FP8X4), w_scales[:, cols], packed[:])
+            nc.vector.quantize_mx(slot_codes[:, cols].bitcast(FP8X4), w_scales[:, cols], packed[:])
 
-        picked_tag = ["neg_q2_codes0", "log_den1", "q_bf0", "part1"]
-        packed_tag = ["neg_logit0", "neg_logit1", None, None]
+        early_packed = sbuf("early_packed", [P, 2 * I], BF16, tag="val_pool1")
+        v_packed = [early_packed[:, 0:I], early_packed[:, I : 2 * I], sbuf("v_packed2", [P, I], BF16)[:], sbuf("v_packed3", [P, I], BF16)[:]]
         turn_bank = ["bank_x0", "bank_x1", "bank_x2", "bank_a0"]
-        acc_bank = ["bank_a1", "bank_x0", "bank_x1", "bank_x2"]
         v_mx = []
         for r in range(PACK):
-            picked = sbuf(f"picked{r}", [P, I], BF16, tag=picked_tag[r])
-            nc.vector.tensor_copy(picked[:], val_pool[r][:].indirect(offsets[:]))
-            packed = turn(f"v{r}", picked, turn_bank[r], packed_tag[r])
-            codes = sbuf(f"v_codes{r}", [P, P], U32)
+            turn(f"v{r}", picked[r], turn_bank[r], v_packed[r])
+            codes = slot_codes[:, Q + r * P : Q + (r + 1) * P]
             scales = sbuf(f"v_scales{r}", [P, P], U8)
-            nc.vector.quantize_mx(codes[:].bitcast(FP8X4), scales[:], packed[:])
+            nc.vector.quantize_mx(codes.bitcast(FP8X4), scales[:], v_packed[r])
             v_mx.append((codes, scales))
 
-        result = sbuf("result", [P, PACK, Q], F32)
         out_rows = out_0.rearrange("(p r) q -> p r q", r=PACK)
-        for r in range(PACK):
-            acc = ps.tile([P, Q], F32, name=f"acc{r}", tag=acc_bank[r])
-            codes, scales = v_mx[r]
-            nc.tensor.matmul_mx(
-                acc[:], lhsT=codes[:].bitcast(FP8X4), lhsT_scale=scales[:],
-                rhs=w_codes[:].bitcast(FP8X4), rhs_scale=w_scales[:], start=True, stop=True,
-            )
-            nc.scalar.copy(result[:, r, :], acc[:])
-            nc.sync.dma_start(out_rows[:, r, :], result[:, r, :])
-
-        result_bf = sbuf("result_bf", [P, Q, PACK], BF16)
-        nc.vector.tensor_copy(result_bf[:], result[:].rearrange("p r q -> p q r"))
         out_codes = sbuf("out_codes", [P, Q], U32)
         out_scales = sbuf("out_scales", [P, Q], U8)
-        nc.vector.quantize_mx(out_codes[:].bitcast(FP8X4), out_scales[:], result_bf[:].rearrange("p q r -> p (q r)"))
+        acc = [ps.tile([P, PACK, P], F32, name=f"acc{h}", tag=f"bank_x{h}") for h in range(HALVES)]
+        for r in range(PACK):
+            codes, scales = v_mx[r]
+            for h in range(HALVES):
+                cols = slice(h * P, (h + 1) * P)
+                nc.tensor.matmul_mx(
+                    acc[h][:, r, :], lhsT=codes.bitcast(FP8X4), lhsT_scale=scales[:],
+                    rhs=slot_codes[:, cols].bitcast(FP8X4), rhs_scale=w_scales[:, cols], start=True, stop=True,
+                )
+        result = [sbuf(f"result{h}", [P, PACK, P], F32) for h in range(HALVES)]
+        result_bf = [sbuf(f"result_bf{h}", [P, P, PACK], BF16) for h in range(HALVES)]
+        nc.vector.tensor_copy(result_bf[0][:], acc[0][:].rearrange("p r q -> p q r"))
+        nc.scalar.copy(result[1][:], acc[1][:])
+        nc.vector.tensor_copy(result_bf[1][:], result[1][:].rearrange("p r q -> p q r"))
+        nc.scalar.copy(result[0][:], acc[0][:])
+        nc.sync.dma_start(out_rows[:, :, P:Q], result[1][:])
+        nc.scalar.dma_start(out_rows[:, :, 0:P], result[0][:])
+        for h in range(HALVES):
+            cols = slice(h * P, (h + 1) * P)
+            nc.vector.quantize_mx(out_codes[:, cols].bitcast(FP8X4), out_scales[:, cols], result_bf[h][:].rearrange("p q r -> p (q r)"))
         nc.sync.dma_start(out_1[0].rearrange("p c t -> p (c t)").bitcast(I32), out_codes[:].bitcast(I32))
         for quad in range(4):
-            queue = nc.scalar if quad % 2 else nc.sync
-            queue.dma_start(
+            nc.sync.dma_start(
                 out_2[0][4 * quad : 4 * quad + 4, :].bitcast(I32),
                 out_scales[32 * quad : 32 * quad + 4, :].bitcast(I32),
             )

@@ -127,10 +127,10 @@ def tile_attend_alikescores_pl_kernel(tc, query, query2, keys_words, keys_scales
         picked = [sbuf(f"picked{r}", [P, I], BF16) for r in range(PACK)]
         for r in range(PACK):
             nc.vector.tensor_copy(picked[r][:], val_pool[r][:].indirect(offsets[:]))
-        neg_logit = sbuf("neg_logit", [P, HALVES * I], F32, tag="val_pool1")
+        neg_logit = sbuf("neg_logit", [P, HALVES * I], F32)
         inv_z = sbuf("inv_z", [P, HALVES], F32, tag="val_pool2")
         for h in range(HALVES):
-            nc.vector.tensor_tensor(neg_logit[:, h * I : (h + 1) * I], neg_half_a[h][:], log_den[h][:], ALU.add)
+            nc.gpsimd.tensor_tensor(neg_logit[:, h * I : (h + 1) * I], neg_half_a[h][:], log_den[h][:], ALU.add)
         for h in range(HALVES):
             nc.scalar.activation(part[h][:], neg_logit[:, h * I : (h + 1) * I], ACT.Exp, bias=shift[h][:], scale=-1.0, accum_out=z[:, h : h + 1])
         nc.vector.reciprocal(inv_z[:], z[:])
@@ -155,7 +155,7 @@ def tile_attend_alikescores_pl_kernel(tc, query, query2, keys_words, keys_scales
             cols = slice(h * P, (h + 1) * P)
             nc.vector.quantize_mx(slot_codes[:, cols].bitcast(FP8X4), w_scales[:, cols], packed[:])
 
-        early_packed = sbuf("early_packed", [P, 2 * I], BF16, tag="val_pool1")
+        early_packed = sbuf("early_packed", [P, 2 * I], BF16, tag="neg_logit")
         v_packed = [early_packed[:, 0:I], early_packed[:, I : 2 * I], sbuf("v_packed2", [P, I], BF16)[:], sbuf("v_packed3", [P, I], BF16)[:]]
         turn_bank = ["bank_x0", "bank_x1", "bank_x2", "bank_a0"]
         v_mx = []
@@ -191,7 +191,8 @@ def tile_attend_alikescores_pl_kernel(tc, query, query2, keys_words, keys_scales
             nc.vector.quantize_mx(out_codes[:, cols].bitcast(FP8X4), out_scales[:, cols], result_bf[h][:].rearrange("p q r -> p (q r)"))
         nc.sync.dma_start(out_1[0].rearrange("p c t -> p (c t)").bitcast(I32), out_codes[:].bitcast(I32))
         for quad in range(4):
-            nc.sync.dma_start(
+            queue = nc.scalar if quad % 2 else nc.sync
+            queue.dma_start(
                 out_2[0][4 * quad : 4 * quad + 4, :].bitcast(I32),
                 out_scales[32 * quad : 32 * quad + 4, :].bitcast(I32),
             )

@@ -106,9 +106,9 @@ def tile_attend_alikescores_pl_kernel(tc, query, query2, keys_words, keys_scales
         for t in range(PACK):
             nc.tensor.transpose(os_rows[:, t, :], os_col[:, t : t + 1].to_broadcast([P, P]), ident[:])
 
-        neg_half_a = [sbuf(f"neg_half_a{h}", [P, I], F32, tag=["neg_q2_bf1", "val_pool0"][h]) for h in range(HALVES)]
+        neg_half_a = [sbuf(f"neg_half_a{h}", [P, I], F32, tag=["neg_q2_bf1", None][h]) for h in range(HALVES)]
         shift = [sbuf(f"shift{h}", [P, 1], F32) for h in range(HALVES)]
-        half_dl0 = sbuf("half_dl0", [P, I], F32)
+        dl0 = sbuf("dl0", [P, I], F32)
         dl_sq = [sbuf(f"dl_sq{h}", [P, I], F32) for h in range(HALVES)]
         log_den = [sbuf(f"log_den{h}", [P, I], F32) for h in range(HALVES)]
         part = [sbuf(f"part{h}", [P, I], F32) for h in range(HALVES)]
@@ -116,14 +116,14 @@ def tile_attend_alikescores_pl_kernel(tc, query, query2, keys_words, keys_scales
         w_bf = [sbuf(f"w_bf{h}", [P, I], BF16) for h in range(HALVES)]
 
         nc.vector.tensor_scalar(neg_half_a[0][:], a0[:], -0.5, None, ALU.mult, ALU.min, accum_out=shift[0][:])
-        nc.vector.scalar_tensor_tensor(half_dl0[:], neg_b0[:], -0.5, neg_half_a[0][:], ALU.mult, ALU.add)
-        a1 = ps.tile([P, I], F32, name="a1", tag="bank_neg_b0")
+        nc.vector.scalar_tensor_tensor(dl0[:], neg_half_a[0][:], -2.0, neg_b0[:], ALU.mult, ALU.add)
+        nc.vector.scalar_tensor_tensor(dl_sq[0][:], dl0[:], sharp_col[:, 0:1], dl0[:], ALU.mult, ALU.mult)
+        a1 = ps.tile([P, I], F32, name="a1", tag="bank_a0")
         score_pass(a1, q_mx[1], True, True)
         nc.vector.tensor_scalar(neg_half_a[1][:], a1[:], -0.5, None, ALU.mult, ALU.min, accum_out=shift[1][:])
-        nc.scalar.activation(dl_sq[0][:], half_dl0[:], ACT.Square, scale=2.0)
-        nc.scalar.activation(dl_sq[1][:], dl1[:], ACT.Square)
-        for h in range(HALVES):
-            nc.scalar.activation(log_den[h][:], dl_sq[h][:], ACT.Ln, bias=1.0, scale=sharp_col[:, h : h + 1])
+        nc.scalar.activation(dl_sq[1][:], dl1[:], ACT.Square, bias=warm_out[:])
+        nc.scalar.activation(log_den[0][:], dl_sq[0][:], ACT.Ln, bias=1.0)
+        nc.scalar.activation(log_den[1][:], dl_sq[1][:], ACT.Ln, bias=1.0, scale=sharp_col[:, 1:2])
         picked = [sbuf(f"picked{r}", [P, I], BF16) for r in range(PACK)]
         for r in range(PACK):
             nc.vector.tensor_copy(picked[r][:], val_pool[r][:].indirect(offsets[:]))
@@ -169,23 +169,20 @@ def tile_attend_alikescores_pl_kernel(tc, query, query2, keys_words, keys_scales
         out_rows = out_0.rearrange("(p r) q -> p r q", r=PACK)
         out_codes = sbuf("out_codes", [P, Q], U32)
         out_scales = sbuf("out_scales", [P, Q], U8)
-        acc = [ps.tile([P, PACK, P], F32, name=f"acc{h}", tag=f"bank_x{h}") for h in range(HALVES)]
-        for r in range(PACK):
+        result = sbuf("result", [P, PACK, Q], F32)
+        for r, bank_tag in enumerate(["bank_x0", "bank_x1", "bank_x2", "bank_neg_b0"]):
             codes, scales = v_mx[r]
-            for h in range(HALVES):
-                cols = slice(h * P, (h + 1) * P)
-                nc.tensor.matmul_mx(
-                    acc[h][:, r, :], lhsT=codes.bitcast(FP8X4), lhsT_scale=scales[:],
-                    rhs=slot_codes[:, cols].bitcast(FP8X4), rhs_scale=w_scales[:, cols], start=True, stop=True,
-                )
-        result = [sbuf(f"result{h}", [P, PACK, P], F32) for h in range(HALVES)]
+            acc = ps.tile([P, Q], F32, name=f"acc{r}", tag=bank_tag)
+            nc.tensor.matmul_mx(
+                acc[:], lhsT=codes.bitcast(FP8X4), lhsT_scale=scales[:],
+                rhs=slot_codes[:, 0:Q].bitcast(FP8X4), rhs_scale=w_scales[:], start=True, stop=True,
+            )
+            nc.scalar.copy(result[:, r, :], acc[:])
+        nc.sync.dma_start(out_rows[:, 0 : PACK - 1, :], result[:, 0 : PACK - 1, :])
+        nc.scalar.dma_start(out_rows[:, PACK - 1, :], result[:, PACK - 1, :])
         result_bf = [sbuf(f"result_bf{h}", [P, P, PACK], BF16) for h in range(HALVES)]
-        nc.vector.tensor_copy(result_bf[0][:], acc[0][:].rearrange("p r q -> p q r"))
-        nc.scalar.copy(result[1][:], acc[1][:])
-        nc.vector.tensor_copy(result_bf[1][:], result[1][:].rearrange("p r q -> p q r"))
-        nc.scalar.copy(result[0][:], acc[0][:])
-        nc.sync.dma_start(out_rows[:, :, P:Q], result[1][:])
-        nc.scalar.dma_start(out_rows[:, :, 0:P], result[0][:])
+        for h in range(HALVES):
+            nc.vector.tensor_copy(result_bf[h][:], result[:, :, h * P : (h + 1) * P].rearrange("p r q -> p q r"))
         for h in range(HALVES):
             cols = slice(h * P, (h + 1) * P)
             nc.vector.quantize_mx(out_codes[:, cols].bitcast(FP8X4), out_scales[:, cols], result_bf[h][:].rearrange("p q r -> p (q r)"))

@@ -72,10 +72,10 @@ def tile_attend_alikescores_pl_kernel(tc, query, query2, keys_words, keys_scales
         nc.vector.tensor_copy(key_words[:], key_word_pool[:].indirect(offsets[:]))
 
         def quantise_queries(name, raw, sign):
-            view = raw[:].rearrange("p t q -> p q t")
+            view = raw[:].rearrange("p t (h c i) -> p h c t i", h=HALVES, i=PACK)
             rounded = [sbuf(f"{name}_bf{h}", [P, P, PACK], BF16) for h in range(HALVES)]
-            nc.vector.tensor_scalar(rounded[0][:], view[:, 0:P, :], sign, None, ALU.mult)
-            nc.scalar.activation(rounded[1][:], view[:, P:Q, :], ACT.Copy, scale=sign)
+            nc.vector.tensor_scalar(rounded[0][:].rearrange("p (c i) t -> p c t i", i=PACK), view[:, 0], sign, None, ALU.mult)
+            nc.scalar.activation(rounded[1][:].rearrange("p (c i) t -> p c t i", i=PACK), view[:, 1], ACT.Copy, scale=sign)
             operands = []
             for h in range(HALVES):
                 codes = sbuf(f"{name}_codes{h}", [P, P], U32)
@@ -182,7 +182,10 @@ def tile_attend_alikescores_pl_kernel(tc, query, query2, keys_words, keys_scales
         nc.scalar.dma_start(out_rows[:, PACK - 1, :], result[:, PACK - 1, :])
         result_bf = [sbuf(f"result_bf{h}", [P, P, PACK], BF16) for h in range(HALVES)]
         for h in range(HALVES):
-            nc.vector.tensor_copy(result_bf[h][:], result[:, :, h * P : (h + 1) * P].rearrange("p r q -> p q r"))
+            nc.vector.tensor_copy(
+                result_bf[h][:].rearrange("p (c i) r -> p c r i", i=PACK),
+                result[:, :, h * P : (h + 1) * P].rearrange("p r (c i) -> p c r i", i=PACK),
+            )
         for h in range(HALVES):
             cols = slice(h * P, (h + 1) * P)
             nc.vector.quantize_mx(out_codes[:, cols].bitcast(FP8X4), out_scales[:, cols], result_bf[h][:].rearrange("p q r -> p (q r)"))

from contextlib import ExitStack

import concourse.mybir as mybir
from concourse.masks import make_identity

D, E, T, I, Q = 512, 512, 2048, 512, 256
FLOPS = 2 * (2 * D * Q * I + I * E * Q)

F32 = mybir.dt.float32
BF16 = mybir.dt.bfloat16
I32 = mybir.dt.int32
U32 = mybir.dt.uint32
U16 = mybir.dt.uint16
U8 = mybir.dt.uint8
FP8X4 = mybir.dt.float8_e4m3fn_x4
ALU = mybir.AluOpType
ACT = mybir.ActivationFunctionType

P = 128
PACK = 4
HALVES = Q // P


def tile_attend_alikescores_pl_kernel(tc, query, query2, keys_words, keys_scales, sharp, slot_factor, vals, offs, out_0, out_1, out_2):
    nc = tc.nc
    with ExitStack() as ctx:
        sb = ctx.enter_context(tc.tile_pool(name="sb", bufs=1))
        ps = ctx.enter_context(tc.psum_pool(name="ps", bufs=1))

        def sbuf(name, shape, dtype, tag=None):
            return sb.tile(shape, dtype, name=name, tag=tag or name, align_bytes=64)

        offsets = sb.tile([P, I // 16], U16, name="offsets")
        nc.sync.dma_start(offsets[:], offs)

        q_raw = sbuf("q_raw", [P, PACK, Q], F32)
        nc.sync.dma_start(q_raw[:], query.rearrange("(p t) q -> p t q", t=PACK))
        key_scale_pool = sbuf("key_scale_pool", [P, T], U8)
        nc.gpsimd.memset(key_scale_pool[:].bitcast(I32), 0)
        for quad in range(4):
            nc.sync.dma_start(
                key_scale_pool[32 * quad : 32 * quad + 4, :].bitcast(I32),
                keys_scales[0][4 * quad : 4 * quad + 4, :].bitcast(I32),
            )
        key_word_pool = sbuf("key_word_pool", [P, T], U32)
        nc.sync.dma_start(key_word_pool[:].bitcast(I32), keys_words[0].rearrange("p n t -> p (n t)").bitcast(I32))
        q2_raw = sbuf("q2_raw", [P, PACK, Q], F32)
        nc.sync.dma_start(q2_raw[:], query2.rearrange("(p t) q -> p t q", t=PACK))
        sharp_col = sbuf("sharp_col", [P, HALVES], F32)
        with nc.allow_non_contiguous_dma(reason="one value a partition"):
            nc.sync.dma_start(sharp_col[:], sharp.rearrange("(h p) o -> p (h o)", p=P))

        val_pool = [sbuf(f"val_pool{r}", [P, T], F32) for r in range(PACK)]
        val_rows = vals.rearrange("(p r) t -> p r t", r=PACK)
        nc.sync.dma_start(val_pool[0][:], val_rows[:, 0, :])
        os_col = sbuf("os_col", [P, PACK], F32)
        nc.sync.dma_start(os_col[:], slot_factor.rearrange("o (s t) -> s (o t)", t=PACK))
        for r in range(1, PACK):
            nc.sync.dma_start(val_pool[r][:], val_rows[:, r, :])

        ident = sbuf("ident", [P, P], F32)
        make_identity(nc, ident[:])

        warm_in = sbuf("warm_in", [P, 1], F32)
        warm_out = sbuf("warm_out", [P, 1], F32)
        nc.vector.memset(warm_in[:], 1.0)
        nc.scalar.activation(warm_out[:], warm_in[:], ACT.Ln)

        key_scales = sbuf("key_scales", [P, I], U8)
        nc.vector.tensor_copy(key_scales[:], key_scale_pool[:].indirect(offsets[:]))
        key_words = sbuf("key_words", [P, I], U32)
        nc.vector.tensor_copy(key_words[:], key_word_pool[:].indirect(offsets[:]))

        def quantise_queries(name, raw, sign):
            view = raw[:].rearrange("p t (h c i) -> p h c t i", h=HALVES, i=PACK)
            rounded = [sbuf(f"{name}_bf{h}", [P, P, PACK], BF16) for h in range(HALVES)]
            nc.vector.tensor_scalar(rounded[0][:].rearrange("p (c i) t -> p c t i", i=PACK), view[:, 0], sign, None, ALU.mult)
            nc.scalar.activation(rounded[1][:].rearrange("p (c i) t -> p c t i", i=PACK), view[:, 1], ACT.Copy, scale=sign)
            operands = []
            for h in range(HALVES):
                codes = sbuf(f"{name}_codes{h}", [P, P], U32)
                scales = sbuf(f"{name}_scales{h}", [P, P], U8)
                nc.vector.quantize_mx(codes[:].bitcast(FP8X4), scales[:], rounded[h][:].rearrange("p q t -> p (q t)"))
                operands.append((codes, scales))
            return operands

        def score_pass(bank, operand, start, stop):
            codes, scales = operand
            nc.tensor.matmul_mx(
                bank[:], lhsT=codes[:].bitcast(FP8X4), lhsT_scale=scales[:],
                rhs=key_words[:].bitcast(FP8X4), rhs_scale=key_scales[:], start=start, stop=stop,
            )

        q_mx = quantise_queries("q", q_raw, 1.0)
        neg_q2_mx = quantise_queries("neg_q2", q2_raw, -1.0)

        a0 = ps.tile([P, I], F32, name="bank_a0")
        neg_b0 = ps.tile([P, I], F32, name="bank_neg_b0")
        dl1 = ps.tile([P, I], F32, name="bank_dl1")
        score_pass(a0, q_mx[0], True, True)
        score_pass(neg_b0, neg_q2_mx[0], True, True)
        score_pass(dl1, neg_q2_mx[1], True, False)
        score_pass(dl1, q_mx[1], False, True)

        os_rows = ps.tile([P, PACK, P], F32, name="os_rows")
        for t in range(PACK):
            nc.tensor.transpose(os_rows[:, t, :], os_col[:, t : t + 1].to_broadcast([P, P]), ident[:])

        neg_half_a = [sbuf(f"neg_half_a{h}", [P, I], F32, tag=["neg_q2_bf1", None][h]) for h in range(HALVES)]
        shift = [sbuf(f"shift{h}", [P, 1], F32) for h in range(HALVES)]
        dl0 = sbuf("dl0", [P, I], F32)
        dl_sq = [sbuf(f"dl_sq{h}", [P, I], F32) for h in range(HALVES)]
        log_den = [sbuf(f"log_den{h}", [P, I], F32) for h in range(HALVES)]
        part = [sbuf(f"part{h}", [P, I], F32) for h in range(HALVES)]
        z = sbuf("z", [P, HALVES], F32)
        w_bf = [sbuf(f"w_bf{h}", [P, I], BF16) for h in range(HALVES)]

        nc.vector.tensor_scalar(neg_half_a[0][:], a0[:], -0.5, None, ALU.mult, ALU.min, accum_out=shift[0][:])
        nc.vector.scalar_tensor_tensor(dl0[:], neg_half_a[0][:], -2.0, neg_b0[:], ALU.mult, ALU.add)
        nc.vector.scalar_tensor_tensor(dl_sq[0][:], dl0[:], sharp_col[:, 0:1], dl0[:], ALU.mult, ALU.mult)
        a1 = ps.tile([P, I], F32, name="a1", tag="bank_a0")
        score_pass(a1, q_mx[1], True, True)
        nc.vector.tensor_scalar(neg_half_a[1][:], a1[:], -0.5, None, ALU.mult, ALU.min, accum_out=shift[1][:])
        nc.scalar.activation(dl_sq[1][:], dl1[:], ACT.Square, bias=warm_out[:])
        nc.scalar.activation(log_den[0][:], dl_sq[0][:], ACT.Ln, bias=1.0)
        nc.scalar.activation(log_den[1][:], dl_sq[1][:], ACT.Ln, bias=1.0, scale=sharp_col[:, 1:2])
        picked = [sbuf(f"picked{r}", [P, I], BF16) for r in range(PACK)]
        for r in range(PACK):
            nc.vector.tensor_copy(picked[r][:], val_pool[r][:].indirect(offsets[:]))
        neg_logit = sbuf("neg_logit", [P, HALVES * I], F32)
        inv_z = sbuf("inv_z", [P, HALVES], F32, tag="val_pool2")
        for h in range(HALVES):
            nc.gpsimd.tensor_tensor(neg_logit[:, h * I : (h + 1) * I], neg_half_a[h][:], log_den[h][:], ALU.add)
        for h in range(HALVES):
            nc.scalar.activation(part[h][:], neg_logit[:, h * I : (h + 1) * I], ACT.Exp, bias=shift[h][:], scale=-1.0, accum_out=z[:, h : h + 1])
        nc.vector.reciprocal(inv_z[:], z[:])
        for h in range(HALVES):
            nc.vector.scalar_tensor_tensor(
                w_bf[h][:].rearrange("q (s t) -> q s t", t=PACK), part[h][:].rearrange("q (s t) -> q s t", t=PACK),
                inv_z[:, h : h + 1], os_rows[:].rearrange("q t s -> q s t"), ALU.mult, ALU.mult,
            )

        def turn(name, rows_bf, bank_tag, packed):
            words = rows_bf[:].bitcast(F32)
            turned = ps.tile([P, 2, P], F32, name=f"{name}_turned", tag=bank_tag)
            for u in range(2):
                nc.tensor.transpose(turned[:, u, :], words[:, u : 2 * P : 2], ident[:])
            nc.scalar.copy(packed.bitcast(F32).rearrange("s (c u) -> s c u", u=2), turned[:].rearrange("s u c -> s c u"))

        slot_codes = sbuf("slot_codes", [P, Q + E], U32, tag="val_pool3")
        w_scales = sbuf("w_scales", [P, Q], U8)
        for h, bank_tag in enumerate(["bank_neg_b0", "bank_dl1"]):
            packed = sbuf(f"w_packed{h}", [P, I], BF16)
            turn(f"w{h}", w_bf[h], bank_tag, packed[:])
            cols = slice(h * P, (h + 1) * P)
            nc.vector.quantize_mx(slot_codes[:, cols].bitcast(FP8X4), w_scales[:, cols], packed[:])

        early_packed = sbuf("early_packed", [P, 2 * I], BF16, tag="neg_logit")
        v_packed = [early_packed[:, 0:I], early_packed[:, I : 2 * I], sbuf("v_packed2", [P, I], BF16)[:], sbuf("v_packed3", [P, I], BF16)[:]]
        turn_bank = ["bank_x0", "bank_x1", "bank_x2", "bank_a0"]
        v_mx = []
        for r in range(PACK):
            turn(f"v{r}", picked[r], turn_bank[r], v_packed[r])
            codes = slot_codes[:, Q + r * P : Q + (r + 1) * P]
            scales = sbuf(f"v_scales{r}", [P, P], U8)
            nc.vector.quantize_mx(codes.bitcast(FP8X4), scales[:], v_packed[r])
            v_mx.append((codes, scales))

        out_rows = out_0.rearrange("(p r) q -> p r q", r=PACK)
        out_codes = sbuf("out_codes", [P, Q], U32)
        out_scales = sbuf("out_scales", [P, Q], U8)
        result = sbuf("result", [P, PACK, Q], F32)
        for r, bank_tag in enumerate(["bank_x0", "bank_x1", "bank_x2", "bank_neg_b0"]):
            codes, scales = v_mx[r]
            acc = ps.tile([P, Q], F32, name=f"acc{r}", tag=bank_tag)
            nc.tensor.matmul_mx(
                acc[:], lhsT=codes.bitcast(FP8X4), lhsT_scale=scales[:],
                rhs=slot_codes[:, 0:Q].bitcast(FP8X4), rhs_scale=w_scales[:], start=True, stop=True,
            )
            nc.scalar.copy(result[:, r, :], acc[:])
        nc.sync.dma_start(out_rows[:, 0 : PACK - 1, :], result[:, 0 : PACK - 1, :])
        nc.scalar.dma_start(out_rows[:, PACK - 1, :], result[:, PACK - 1, :])
        result_bf = [sbuf(f"result_bf{h}", [P, P, PACK], BF16) for h in range(HALVES)]
        for h in range(HALVES):
            nc.vector.tensor_copy(
                result_bf[h][:].rearrange("p (c i) r -> p c r i", i=PACK),
                result[:, :, h * P : (h + 1) * P].rearrange("p r (c i) -> p c r i", i=PACK),
            )
        for h in range(HALVES):
            cols = slice(h * P, (h + 1) * P)
            nc.vector.quantize_mx(out_codes[:, cols].bitcast(FP8X4), out_scales[:, cols], result_bf[h][:].rearrange("p q r -> p (q r)"))
        nc.sync.dma_start(out_1[0].rearrange("p c t -> p (c t)").bitcast(I32), out_codes[:].bitcast(I32))
        for quad in range(4):
            queue = nc.scalar if quad % 2 else nc.sync
            queue.dma_start(
                out_2[0][4 * quad : 4 * quad + 4, :].bitcast(I32),
                out_scales[32 * quad : 32 * quad + 4, :].bitcast(I32),
            )
